import numpy as np
import ml_dtypes


def mxq(x, axis, fmt="e4m3"):
    dtype, down = {"e4m3": (ml_dtypes.float8_e4m3fn, 7), "e5m2": (ml_dtypes.float8_e5m2, 14)}[fmt]
    v = np.moveaxis(np.asarray(x, np.float32).astype(ml_dtypes.bfloat16).astype(np.float64), axis, -1)
    blocks = v.reshape(v.shape[:-1] + (-1, 32))
    amax = np.abs(blocks).max(-1, keepdims=True)
    byte = np.maximum(np.where(amax > 0, np.frexp(amax)[1] - 1 + 127, 0) - down, 1)
    scale = np.exp2(byte - 127.0)
    codes = (blocks / scale).astype(np.float32).astype(dtype).astype(np.float64)
    return np.moveaxis((codes * scale).reshape(v.shape), -1, axis)


WIDE = False


def mx_kscale(k):
    if not WIDE:
        return np.ones(k)
    levels = np.array([10, -10, 5, -5, 0])
    if k % 512:
        return np.exp2(np.random.permutation(np.resize(levels, k // 32))).repeat(32)
    a = np.empty((k // 512, 16))
    for p in range(k // 512):
        a[p, :8] = np.random.permutation(np.resize(levels, 8))
        for g in range(8):
            far = levels[np.abs(levels - a[p, g]) >= 10]
            a[p, g + 8] = far[np.random.randint(len(far))]
    return np.exp2(a.ravel()).repeat(32)


def f64(x):
    return np.asarray(x).astype(np.float64)


def striped(idx):
    return np.tile(idx.reshape(-1, 16).T, (8, 1)).astype(np.uint16)


def unstriped(offs):
    return offs[:16].T.reshape(-1).astype(np.int64)


E2M1 = np.array([0.0, 0.5, 1.0, 1.5, 2.0, 3.0, 4.0, 6.0, -0.0, -0.5, -1.0, -1.5, -2.0, -3.0, -4.0, -6.0])


def pack_weight(w, fmt):
    k, n = w.shape
    w = f64(np.asarray(w, np.float32).astype(ml_dtypes.bfloat16)).reshape(k // 32, 32, n)
    amax = np.abs(w).max(1)
    if fmt == "e4m3":
        byte = np.frexp(amax)[1] - 1 + 127 - 7
    else:
        mant, ex = np.frexp(amax / 6.0)
        byte = np.where(mant > 0.5, ex, ex - 1) + 127
    byte = np.clip(np.where(amax > 0, byte, 1), 1, 254)
    scaled = (w * np.exp2(127.0 - byte)[:, None, :]).reshape(k, n).astype(np.float32)
    by_word = np.ascontiguousarray(scaled.reshape(k // 512, 128, 4, n).transpose(0, 1, 3, 2))
    if fmt == "e4m3":
        words = by_word.astype(ml_dtypes.float8_e4m3fn).view(np.uint8)
    else:
        c = by_word.astype(ml_dtypes.float4_e2m1fn).view(np.uint8) & 0xF
        words = (c[..., 0::2] | (c[..., 1::2] << 4)).reshape(k // 512, 128, 2 * n)
    return np.ascontiguousarray(words), np.ascontiguousarray(byte.astype(np.uint8).reshape(k // 512, 16, n))


def unpack_weight(words, scales, fmt):
    g, _, n = scales.shape
    words = np.ascontiguousarray(words).reshape(g, 128, n, -1)
    if fmt == "e4m3":
        vals = words.view(ml_dtypes.float8_e4m3fn).astype(np.float64)
    else:
        nib = np.empty((g, 128, n, 4), np.uint8)
        nib[..., 0::2] = words & 0xF
        nib[..., 1::2] = words >> 4
        vals = E2M1[nib]
    vals = vals * np.repeat(np.exp2(scales.astype(np.float64) - 127.0), 8, axis=1)[..., None]
    return vals.transpose(0, 1, 3, 2).reshape(g * 512, n)


def gelu(v):
    return 0.5 * v * (1.0 + np.tanh(np.sqrt(2.0 / np.pi) * (v + 0.044715 * v**3)))


K, T, S, S2 = 1024, 4096, 1024, 512


def setup_inputs():
    n = np.random.standard_normal
    s = mx_kscale(K)[:, None]
    d = {}
    d["tab_words"], d["tab_scales"] = pack_weight(n((K, T)) * s, "e4m3")
    d["offs"] = striped(np.random.permutation(T)[:S])
    d["offs2"] = striped(np.random.permutation(T)[:S2])
    d["w1"] = (1.5 * n((K, K)) / s / K ** 0.5).astype(np.float32)
    d["gain"] = (np.exp(0.4 * n(K)) / s[:, 0] / K ** 0.5).astype(np.float32)
    d["w4_words"], d["w4_scales"] = pack_weight(n((K, S)) / s / K ** 0.5, "e2m1")
    d["urg"] = np.exp(0.4 * n(S2)).astype(np.float32)
    return d


def reference(tab_words, tab_scales, offs, offs2, w1, gain, w4_words, w4_scales, urg):
    TW = unpack_weight(tab_words, tab_scales, "e4m3")
    v = TW[:, unstriped(offs)]
    v2 = TW[:, unstriped(offs2)]
    w4 = unpack_weight(w4_words, w4_scales, "e2m1")
    x = mxq(f64(w1), 0, "e4m3").T @ v
    h = 0.5 * x * (1.0 + np.tanh(0.7978845608 * (x + 0.044715 * x ** 3)))
    h = h * f64(gain)[:, None]
    e = v2.T @ mxq(h, 0, "e4m3")
    f = v2.T @ w4
    return np.square(e - f) * f64(urg)[:, None]

@@ -1,0 +1,277 @@
+from contextlib import ExitStack
+
+import concourse.mybir as mybir
+
+K, T, S, S2 = 1024, 4096, 1024, 512
+FLOPS = 2 * K * K * S + 2 * 2 * K * S2 * S
+
+F32 = mybir.dt.float32
+BF16 = mybir.dt.bfloat16
+I32 = mybir.dt.int32
+U32 = mybir.dt.uint32
+U16 = mybir.dt.uint16
+U8 = mybir.dt.uint8
+FP8X4 = mybir.dt.float8_e4m3fn_x4
+FP4X4 = mybir.dt.float4_e2m1fn_x4
+ACT = mybir.ActivationFunctionType
+MULT = mybir.AluOpType.mult
+
+P = 128
+PACK = 4
+KP = P * PACK
+PASSES = K // KP
+HALF = 512
+CHUNK = 256
+MT = S2 // P
+
+
+def tile_list_graft_mismatch_score_kernel(
+    tc, tab_words, tab_scales, offs, offs2, w1, gain, w4_words, w4_scales, urg, out
+):
+    nc = tc.nc
+    with ExitStack() as ctx:
+        keep = ctx.enter_context(tc.tile_pool(name="keep", bufs=1))
+        shared = ctx.enter_context(tc.tile_pool(name="shared", bufs=1))
+        ring = ctx.enter_context(tc.tile_pool(name="ring", bufs=4))
+        psum = ctx.enter_context(tc.psum_pool(name="psum", bufs=1))
+
+        def held(shape, dtype, name):
+            return keep.tile(shape, dtype, name=name, align_bytes=64)
+
+        list2 = keep.tile([P, S2 // 16], U16, name="list2")
+        nc.sync.dma_start(list2[:], offs2)
+        list1 = keep.tile([P, S // 16], U16, name="list1")
+        nc.sync.dma_start(list1[:], offs)
+
+        scale_rows = shared.tile([P, T], U8, name="scale_rows", align_bytes=64, offset=6144)
+        nc.vector.memset(scale_rows[:].bitcast(I32), 0)
+        by_row = tab_scales.rearrange("a (q r) t -> r q a t", r=4)
+        for r in range(4):
+            nc.scalar.dma_start(scale_rows[r:P:16, :].bitcast(I32), by_row[r].bitcast(I32))
+        w4_plane = held([P, PASSES, S], U8, "w4_plane")
+        nc.vector.memset(w4_plane[:].rearrange("p a n -> p (a n)").bitcast(I32), 0)
+        plane1 = held([P, S2 + S], U8, "plane1")
+        nc.vector.memset(plane1[:].bitcast(I32), 0)
+        warm = held([P, 1], F32, "warm")
+        nc.vector.memset(warm[:], 0.0)
+        warm_out = held([P, 1], F32, "warm_out")
+        nc.scalar.activation(warm_out[:], warm[:], ACT.Gelu_apprx_tanh)
+
+        gain_sb = held([P, PASSES, PACK], F32, "gain_sb")
+        nc.gpsimd.dma_start(gain_sb[:], gain.rearrange("(b p t) -> p b t", p=P, t=PACK))
+        tab = []
+        for a in range(PASSES):
+            words = shared.tile([P, T], U32, name=f"tab{a}", align_bytes=64, offset=16384 * (a + 1))
+            nc.sync.dma_start(
+                words[:].bitcast(I32), tab_words[a].rearrange("p t i -> p (t i)").bitcast(I32)
+            )
+            tab.append(words)
+        for q in range(4):
+            nc.gpsimd.dma_start(
+                w4_plane[32 * q : 32 * q + 4, :, :].bitcast(I32),
+                w4_scales[:, 4 * q : 4 * q + 4, :].rearrange("a r n -> r a n").bitcast(I32),
+            )
+        neg_gain = held([P, PASSES, 2, 2], F32, "neg_gain")
+        nc.vector.tensor_scalar(
+            neg_gain[:].rearrange("p b u e -> p b (u e)"), gain_sb[:], -1.0, None, MULT
+        )
+
+        def load_w4(h):
+            words = shared.tile([P, PASSES, 2 * HALF], U8, name=f"w4_{h}", align_bytes=64, offset=49152 + 2048 * h)
+            nc.sync.dma_start(
+                words[:].bitcast(I32),
+                w4_words[:, :, 2 * HALF * h : 2 * HALF * (h + 1)].rearrange("a p n -> p a n").bitcast(I32),
+            )
+            return words
+
+        def load_w1(b, a, c0, width):
+            raw = shared.tile([P, PACK, width], F32, name=f"w1_{b}_{a}", align_bytes=64, offset=8192 * a)
+            src = w1[KP * a : KP * (a + 1), KP * b + c0 : KP * b + c0 + width]
+            nc.sync.dma_start(raw[:], src.rearrange("(p j) c -> p j c", j=PACK))
+            return raw
+
+        w4 = [load_w4(0)]
+        urg_sb = held([P, MT], F32, "urg_sb")
+        with nc.allow_non_contiguous_dma(reason="one urgency value for each partition"):
+            nc.gpsimd.dma_start(urg_sb[:], urg.rearrange("(m p) -> p m", p=P))
+
+        plane0 = held([P, S2 + S], U8, "plane0")
+        nc.vector.tensor_copy(plane0[:, :S2], scale_rows[:].indirect(list2[:]))
+        nc.vector.tensor_copy(plane0[:, S2:], scale_rows[:].indirect(list1[:]))
+        nc.scalar.dma_start(plane1[0:112, :].bitcast(I32), plane0[16:128, :].bitcast(I32))
+        planes = [plane0, plane1]
+        raw0 = [load_w1(0, a, 0, 512) for a in range(PASSES)]
+        v, v2 = [], []
+        for a in range(PASSES):
+            picked2 = held([P, S2], U32, f"v2_{a}")
+            nc.vector.tensor_copy(picked2[:], tab[a][:].indirect(list2[:]))
+            v2.append(picked2)
+            picked = held([P, S], U32, f"v_{a}")
+            nc.vector.tensor_copy(picked[:], tab[a][:].indirect(list1[:]))
+            v.append(picked)
+
+        grouped = [[shared.tile([P, PACK, P, PACK], BF16, name=f"wg{b}{a}", align_bytes=64, offset=51200 + 4096 * (2 * b + 1 - a)) for a in range(PASSES)] for b in range(PASSES)]
+        w1_codes = [[held([P, KP], U32, f"wc{b}{a}") for a in range(PASSES)] for b in range(PASSES)]
+        w1_plane = [[held([P, KP], U8, f"ws{b}{a}") for a in range(PASSES)] for b in range(PASSES)]
+
+        def cast_w1(on_vector, b, a, raw, c0, m0, m1):
+            dst = grouped[b][a][:, :, m0:m1, :].rearrange("p t m j -> p m j t")
+            src = raw[:, :, PACK * m0 - c0 : PACK * m1 - c0].rearrange("p j (m t) -> p m j t", t=PACK)
+            if on_vector:
+                nc.vector.tensor_copy(dst, src)
+            else:
+                nc.scalar.copy(dst, src)
+
+        def quantize_w1(b, a, t0, t1):
+            nc.vector.quantize_mx(
+                out=w1_codes[b][a][:, P * t0 : P * t1].bitcast(FP8X4),
+                scales=w1_plane[b][a][:, P * t0 : P * t1],
+                in_=grouped[b][a][:, t0:t1].rearrange("p t m j -> p (t m j)"),
+            )
+
+        h_codes = [[held([P, HALF], U32, f"hc{b}{h}") for h in range(2)] for b in range(PASSES)]
+        h_plane = [[held([P, HALF], U8, f"hs{b}{h}") for h in range(2)] for b in range(PASSES)]
+        acc = {}
+
+        def f_passes(h, m, tag):
+            bank = psum.tile([P, HALF], F32, name=f"acc{h}{m}", tag=tag)
+            acc[h, m] = bank
+            cols = slice(P * m, P * (m + 1))
+            for a in range(PASSES):
+                nc.tensor.matmul_mx(
+                    out=bank[:],
+                    lhsT=v2[a][:, cols].bitcast(FP8X4),
+                    lhsT_scale=planes[a][:, cols],
+                    rhs=w4[h][:, a, :].bitcast(FP4X4),
+                    rhs_scale=w4_plane[:, a, HALF * h : HALF * (h + 1)],
+                    start=(a == 0),
+                    stop=False,
+                )
+
+        def e_pass(h, m, b, n0, n1, stop):
+            cols = slice(P * m, P * (m + 1))
+            nc.tensor.matmul_mx(
+                out=acc[h, m][:, n0:n1],
+                lhsT=v2[b][:, cols].bitcast(FP8X4),
+                lhsT_scale=planes[b][:, cols],
+                rhs=h_codes[b][h][:, n0:n1].bitcast(FP8X4),
+                rhs_scale=h_plane[b][h][:, n0:n1],
+                start=False,
+                stop=stop,
+            )
+
+        squares = {}
+
+        def square(h, m):
+            squares[h, m] = held([P, HALF], F32, f"square{h}{m}")
+            nc.scalar.activation(squares[h, m][:], acc[h, m][:], ACT.Square)
+
+        def finish(h, m):
+            result = held([P, HALF], F32, f"result{h}{m}")
+            nc.vector.tensor_scalar(result[:], squares[h, m][:], urg_sb[:, m : m + 1], None, MULT)
+            nc.sync.dma_start(out[P * m : P * (m + 1), HALF * h : HALF * (h + 1)], result[:])
+
+        steps = [(b, c) for b in range(PASSES) for c in range(S // CHUNK)]
+        gelus, scaled = {}, {}
+
+        def first_product(i):
+            b, c = steps[i]
+            cols = slice(CHUNK * c, CHUNK * (c + 1))
+            gelu = ring.tile([P, 2, CHUNK, 2], F32, name="gelu")
+            gelus[i] = gelu
+            for u in range(2):
+                bank = psum.tile([P, 2, CHUNK], F32, name="x", tag=f"ring{(2 * i + u) % 4 if i < 4 else (2 * i + u - 8) % 3}")
+                for e in range(2):
+                    rows = slice(P * (2 * u + e), P * (2 * u + e + 1))
+                    for a in range(PASSES):
+                        nc.tensor.matmul_mx(
+                            out=bank[:, e, :],
+                            lhsT=w1_codes[b][a][:, rows].bitcast(FP8X4),
+                            lhsT_scale=w1_plane[b][a][:, rows],
+                            rhs=v[a][:, cols].bitcast(FP8X4),
+                            rhs_scale=planes[a][:, S2 + CHUNK * c : S2 + CHUNK * (c + 1)],
+                            start=(a == 0),
+                            stop=(a == PASSES - 1),
+                        )
+                nc.scalar.activation(gelu[:, u], bank[:].rearrange("p e n -> p n e"), ACT.Gelu_apprx_tanh)
+
+        def scale_h(i):
+            b = steps[i][0]
+            h_bf = ring.tile([P, CHUNK, 2, 2], BF16, name="h_bf", align_bytes=64)
+            scaled[i] = h_bf
+            nc.vector.tensor_tensor(
+                h_bf[:],
+                gelus[i][:].rearrange("p u n e -> p n u e"),
+                neg_gain[:, b : b + 1].to_broadcast([P, CHUNK, 2, 2]),
+                MULT,
+            )
+
+        def quantize_h(i):
+            b, c = steps[i]
+            cols = slice(CHUNK * (c % 2), CHUNK * (c % 2 + 1))
+            nc.vector.quantize_mx(
+                out=h_codes[b][c // 2][:, cols].bitcast(FP8X4),
+                scales=h_plane[b][c // 2][:, cols],
+                in_=scaled[i][:].rearrange("p n u e -> p (n u e)"),
+            )
+
+        for m in range(MT):
+            f_passes(0, m, f"acc{m}")
+        cast_w1(False, 0, 0, raw0[0], 0, 0, 128)
+        raw1 = [load_w1(1, 0, 0, 512)]
+        quantize_w1(0, 0, 0, 4)
+        cast_w1(False, 0, 1, raw0[1], 0, 0, 44)
+        cast_w1(True, 0, 1, raw0[1], 0, 44, 128)
+        raw1.append(load_w1(1, 1, 0, 512))
+        quantize_w1(0, 1, 0, 2)
+        quantize_w1(0, 1, 2, 4)
+        w4.append(load_w4(1))
+
+        first_product(0)
+        cast_w1(True, 1, 0, raw1[0], 0, 0, 48)
+        first_product(1)
+        cast_w1(False, 1, 0, raw1[0], 0, 48, 128)
+        scale_h(0)
+        first_product(2)
+        scale_h(1)
+        quantize_h(0)
+        quantize_w1(1, 0, 0, 4)
+        cast_w1(False, 1, 1, raw1[1], 0, 48, 128)
+        cast_w1(True, 1, 1, raw1[1], 0, 0, 48)
+        quantize_h(1)
+        first_product(3)
+        f_passes(1, 0, "ring3")
+        scale_h(2)
+        quantize_w1(1, 1, 0, 4)
+        for m in range(MT):
+            e_pass(0, m, 0, 0, HALF, False)
+        first_product(4)
+        scale_h(3)
+        quantize_h(2)
+        first_product(5)
+        scale_h(4)
+        quantize_h(3)
+        first_product(6)
+        e_pass(1, 0, 0, 0, HALF, False)
+        scale_h(5)
+        quantize_h(4)
+        first_product(7)
+        quantize_h(5)
+        for m in range(MT):
+            e_pass(0, m, 1, 0, HALF, True)
+            square(0, m)
+        scale_h(6)
+        for m in range(1, MT):
+            f_passes(1, m, f"ring{(m + 1) % 3}")
+            e_pass(1, m, 0, 0, HALF, False)
+        scale_h(7)
+        quantize_h(6)
+        for m in range(MT):
+            e_pass(1, m, 1, 0, CHUNK, False)
+        quantize_h(7)
+        for m in range(MT):
+            e_pass(1, m, 1, CHUNK, HALF, True)
+            square(1, m)
+        for h in range(2):
+            for m in range(MT):
+                finish(h, m)

@@ -43,25 +43,30 @@ def tile_list_graft_mismatch_score_kernel(
         list1 = keep.tile([P, S // 16], U16, name="list1")
         nc.sync.dma_start(list1[:], offs)
 
-        scale_rows = shared.tile([P, T], U8, name="scale_rows", align_bytes=64, offset=6144)
+        scale_rows = shared.tile([P, T], U8, name="scale_rows", align_bytes=64, offset=26624)
         nc.vector.memset(scale_rows[:].bitcast(I32), 0)
         by_row = tab_scales.rearrange("a (q r) t -> r q a t", r=4)
         for r in range(4):
             nc.scalar.dma_start(scale_rows[r:P:16, :].bitcast(I32), by_row[r].bitcast(I32))
         w4_plane = held([P, PASSES, S], U8, "w4_plane")
-        nc.vector.memset(w4_plane[:].rearrange("p a n -> p (a n)").bitcast(I32), 0)
+        nc.gpsimd.memset(w4_plane[:].rearrange("p a n -> p (a n)").bitcast(I32), 0)
         plane1 = held([P, S2 + S], U8, "plane1")
         nc.vector.memset(plane1[:].bitcast(I32), 0)
-        warm = held([P, 1], F32, "warm")
+        warm = shared.tile([P, 32], F32, name="warm", align_bytes=64, offset=16384 - 64)
         nc.vector.memset(warm[:], 0.0)
-        warm_out = held([P, 1], F32, "warm_out")
+        warm_out = held([P, 32], F32, "warm_out")
         nc.scalar.activation(warm_out[:], warm[:], ACT.Gelu_apprx_tanh)
 
-        gain_sb = held([P, PASSES, PACK], F32, "gain_sb")
-        nc.gpsimd.dma_start(gain_sb[:], gain.rearrange("(b p t) -> p b t", p=P, t=PACK))
+        gain_sb = shared.tile([P, PASSES, PACK], F32, name="gain_sb", align_bytes=64, offset=51200)
+        nc.scalar.dma_start(gain_sb[:], gain.rearrange("(b p t) -> p b t", p=P, t=PACK))
+        neg_gain = held([P, PASSES, 2, 2], F32, "neg_gain")
+        nc.scalar.activation(
+            neg_gain[:].rearrange("p b u e -> p b (u e)"), gain_sb[:], ACT.Copy, scale=-1.0
+        )
+
         tab = []
         for a in range(PASSES):
-            words = shared.tile([P, T], U32, name=f"tab{a}", align_bytes=64, offset=16384 * (a + 1))
+            words = shared.tile([P, T], U32, name=f"tab{a}", align_bytes=64, offset=32768 * (1 - a))
             nc.sync.dma_start(
                 words[:].bitcast(I32), tab_words[a].rearrange("p t i -> p (t i)").bitcast(I32)
             )
@@ -71,13 +76,9 @@ def tile_list_graft_mismatch_score_kernel(
                 w4_plane[32 * q : 32 * q + 4, :, :].bitcast(I32),
                 w4_scales[:, 4 * q : 4 * q + 4, :].rearrange("a r n -> r a n").bitcast(I32),
             )
-        neg_gain = held([P, PASSES, 2, 2], F32, "neg_gain")
-        nc.vector.tensor_scalar(
-            neg_gain[:].rearrange("p b u e -> p b (u e)"), gain_sb[:], -1.0, None, MULT
-        )
 
         def load_w4(h):
-            words = shared.tile([P, PASSES, 2 * HALF], U8, name=f"w4_{h}", align_bytes=64, offset=49152 + 2048 * h)
+            words = shared.tile([P, PASSES, 2 * HALF], U8, name=f"w4_{h}", align_bytes=64, offset=49152 + 4096 * h)
             nc.sync.dma_start(
                 words[:].bitcast(I32),
                 w4_words[:, :, 2 * HALF * h : 2 * HALF * (h + 1)].rearrange("a p n -> p a n").bitcast(I32),
@@ -85,22 +86,22 @@ def tile_list_graft_mismatch_score_kernel(
             return words
 
         def load_w1(b, a, c0, width):
-            raw = shared.tile([P, PACK, width], F32, name=f"w1_{b}_{a}", align_bytes=64, offset=8192 * a)
+            raw = shared.tile([P, PACK, width], F32, name=f"w1_{b}_{a}_{c0}", align_bytes=64, offset=16384 + 8192 * a + 16 * c0)
             src = w1[KP * a : KP * (a + 1), KP * b + c0 : KP * b + c0 + width]
             nc.sync.dma_start(raw[:], src.rearrange("(p j) c -> p j c", j=PACK))
             return raw
 
         w4 = [load_w4(0)]
-        urg_sb = held([P, MT], F32, "urg_sb")
-        with nc.allow_non_contiguous_dma(reason="one urgency value for each partition"):
-            nc.gpsimd.dma_start(urg_sb[:], urg.rearrange("(m p) -> p m", p=P))
-
+        raw00 = load_w1(0, 0, 0, 512)
         plane0 = held([P, S2 + S], U8, "plane0")
         nc.vector.tensor_copy(plane0[:, :S2], scale_rows[:].indirect(list2[:]))
         nc.vector.tensor_copy(plane0[:, S2:], scale_rows[:].indirect(list1[:]))
         nc.scalar.dma_start(plane1[0:112, :].bitcast(I32), plane0[16:128, :].bitcast(I32))
         planes = [plane0, plane1]
-        raw0 = [load_w1(0, a, 0, 512) for a in range(PASSES)]
+        raw01 = [load_w1(0, 1, c0, 256) for c0 in (0, 256)]
+        urg_sb = shared.tile([P, MT], F32, name="urg_sb", align_bytes=64, offset=51200)
+        with nc.allow_non_contiguous_dma(reason="one urgency value for each partition"):
+            nc.scalar.dma_start(urg_sb[:], urg.rearrange("(m p) -> p m", p=P))
         v, v2 = [], []
         for a in range(PASSES):
             picked2 = held([P, S2], U32, f"v2_{a}")
@@ -110,13 +111,13 @@ def tile_list_graft_mismatch_score_kernel(
             nc.vector.tensor_copy(picked[:], tab[a][:].indirect(list1[:]))
             v.append(picked)
 
-        grouped = [[shared.tile([P, PACK, P, PACK], BF16, name=f"wg{b}{a}", align_bytes=64, offset=51200 + 4096 * (2 * b + 1 - a)) for a in range(PASSES)] for b in range(PASSES)]
+        grouped = [[shared.tile([P, PACK, P, PACK], BF16, name=f"wg{b}{a}", align_bytes=64, offset=53248 + 4096 * (2 * b + 1 - a)) for a in range(PASSES)] for b in range(PASSES)]
         w1_codes = [[held([P, KP], U32, f"wc{b}{a}") for a in range(PASSES)] for b in range(PASSES)]
         w1_plane = [[held([P, KP], U8, f"ws{b}{a}") for a in range(PASSES)] for b in range(PASSES)]
 
         def cast_w1(on_vector, b, a, raw, c0, m0, m1):
-            dst = grouped[b][a][:, :, m0:m1, :].rearrange("p t m j -> p m j t")
-            src = raw[:, :, PACK * m0 - c0 : PACK * m1 - c0].rearrange("p j (m t) -> p m j t", t=PACK)
+            dst = grouped[b][a][:, :, m0:m1, :].rearrange("p t m j -> p m t j")
+            src = raw[:, :, PACK * m0 - c0 : PACK * m1 - c0].rearrange("p j (m t) -> p m t j", t=PACK)
             if on_vector:
                 nc.vector.tensor_copy(dst, src)
             else:
@@ -133,11 +134,12 @@ def tile_list_graft_mismatch_score_kernel(
         h_plane = [[held([P, HALF], U8, f"hs{b}{h}") for h in range(2)] for b in range(PASSES)]
         acc = {}
 
-        def f_passes(h, m, tag):
-            bank = psum.tile([P, HALF], F32, name=f"acc{h}{m}", tag=tag)
-            acc[h, m] = bank
+        def f_passes(h, m, tag, passes=(0, 1)):
+            if passes[0] == 0:
+                acc[h, m] = psum.tile([P, HALF], F32, name=f"acc{h}{m}", tag=tag)
+            bank = acc[h, m]
             cols = slice(P * m, P * (m + 1))
-            for a in range(PASSES):
+            for a in passes:
                 nc.tensor.matmul_mx(
                     out=bank[:],
                     lhsT=v2[a][:, cols].bitcast(FP8X4),
@@ -215,13 +217,15 @@ def tile_list_graft_mismatch_score_kernel(
                 in_=scaled[i][:].rearrange("p n u e -> p (n u e)"),
             )
 
-        for m in range(MT):
-            f_passes(0, m, f"acc{m}")
-        cast_w1(False, 0, 0, raw0[0], 0, 0, 128)
+        for a in range(PASSES):
+            for m in range(MT):
+                f_passes(0, m, f"acc{m}", (a,))
+        cast_w1(False, 0, 0, raw00, 0, 0, 128)
         raw1 = [load_w1(1, 0, 0, 512)]
         quantize_w1(0, 0, 0, 4)
-        cast_w1(False, 0, 1, raw0[1], 0, 0, 44)
-        cast_w1(True, 0, 1, raw0[1], 0, 44, 128)
+        cast_w1(False, 0, 1, raw01[0], 0, 0, 64)
+        cast_w1(False, 0, 1, raw01[1], 256, 64, 92)
+        cast_w1(True, 0, 1, raw01[1], 256, 92, 128)
         raw1.append(load_w1(1, 1, 0, 512))
         quantize_w1(0, 1, 0, 2)
         quantize_w1(0, 1, 2, 4)

@@ -43,7 +43,7 @@ def tile_list_graft_mismatch_score_kernel(
         list1 = keep.tile([P, S // 16], U16, name="list1")
         nc.sync.dma_start(list1[:], offs)
 
-        scale_rows = shared.tile([P, T], U8, name="scale_rows", align_bytes=64, offset=26624)
+        scale_rows = shared.tile([P, T], U8, name="scale_rows", align_bytes=64, offset=28672)
         nc.vector.memset(scale_rows[:].bitcast(I32), 0)
         by_row = tab_scales.rearrange("a (q r) t -> r q a t", r=4)
         for r in range(4):
@@ -57,20 +57,13 @@ def tile_list_graft_mismatch_score_kernel(
         warm_out = held([P, 32], F32, "warm_out")
         nc.scalar.activation(warm_out[:], warm[:], ACT.Gelu_apprx_tanh)
 
-        gain_sb = shared.tile([P, PASSES, PACK], F32, name="gain_sb", align_bytes=64, offset=51200)
+        gain_sb = held([P, PASSES, PACK], F32, "gain_sb")
         nc.scalar.dma_start(gain_sb[:], gain.rearrange("(b p t) -> p b t", p=P, t=PACK))
         neg_gain = held([P, PASSES, 2, 2], F32, "neg_gain")
         nc.scalar.activation(
             neg_gain[:].rearrange("p b u e -> p b (u e)"), gain_sb[:], ACT.Copy, scale=-1.0
         )
 
-        tab = []
-        for a in range(PASSES):
-            words = shared.tile([P, T], U32, name=f"tab{a}", align_bytes=64, offset=32768 * (1 - a))
-            nc.sync.dma_start(
-                words[:].bitcast(I32), tab_words[a].rearrange("p t i -> p (t i)").bitcast(I32)
-            )
-            tab.append(words)
         for q in range(4):
             nc.gpsimd.dma_start(
                 w4_plane[32 * q : 32 * q + 4, :, :].bitcast(I32),
@@ -78,40 +71,52 @@ def tile_list_graft_mismatch_score_kernel(
             )
 
         def load_w4(h):
-            words = shared.tile([P, PASSES, 2 * HALF], U8, name=f"w4_{h}", align_bytes=64, offset=49152 + 4096 * h)
+            words = shared.tile([P, PASSES, 2 * HALF], U8, name=f"w4_{h}", align_bytes=64, offset=55296 if h else 24576)
             nc.sync.dma_start(
                 words[:].bitcast(I32),
                 w4_words[:, :, 2 * HALF * h : 2 * HALF * (h + 1)].rearrange("a p n -> p a n").bitcast(I32),
             )
             return words
 
-        def load_w1(b, a, c0, width):
-            raw = shared.tile([P, PACK, width], F32, name=f"w1_{b}_{a}_{c0}", align_bytes=64, offset=16384 + 8192 * a + 16 * c0)
+        def load_w1(b, a, c0, width, offset):
+            raw = shared.tile([P, PACK, width], F32, name=f"w1_{b}_{a}_{c0}", align_bytes=64, offset=offset)
             src = w1[KP * a : KP * (a + 1), KP * b + c0 : KP * b + c0 + width]
             nc.sync.dma_start(raw[:], src.rearrange("(p j) c -> p j c", j=PACK))
             return raw
 
+        def load_tab(a):
+            words = shared.tile([P, T], U32, name=f"tab{a}", align_bytes=64, offset=38912 * (1 - a))
+            nc.sync.dma_start(
+                words[:].bitcast(I32), tab_words[a].rearrange("p t i -> p (t i)").bitcast(I32)
+            )
+            return words
+
+        tab = [load_tab(0)]
         w4 = [load_w4(0)]
-        raw00 = load_w1(0, 0, 0, 512)
+        raw00 = load_w1(0, 0, 0, 512, 16384)
+        tab.append(load_tab(1))
+
         plane0 = held([P, S2 + S], U8, "plane0")
         nc.vector.tensor_copy(plane0[:, :S2], scale_rows[:].indirect(list2[:]))
         nc.vector.tensor_copy(plane0[:, S2:], scale_rows[:].indirect(list1[:]))
-        nc.scalar.dma_start(plane1[0:112, :].bitcast(I32), plane0[16:128, :].bitcast(I32))
+        nc.sync.dma_start(plane1[0:112, :].bitcast(I32), plane0[16:128, :].bitcast(I32))
         planes = [plane0, plane1]
-        raw01 = [load_w1(0, 1, c0, 256) for c0 in (0, 256)]
-        urg_sb = shared.tile([P, MT], F32, name="urg_sb", align_bytes=64, offset=51200)
-        with nc.allow_non_contiguous_dma(reason="one urgency value for each partition"):
-            nc.scalar.dma_start(urg_sb[:], urg.rearrange("(m p) -> p m", p=P))
+        raw01 = [load_w1(0, 1, 0, 256, 26624), load_w1(0, 1, 256, 256, 30720)]
         v, v2 = [], []
         for a in range(PASSES):
             picked2 = held([P, S2], U32, f"v2_{a}")
             nc.vector.tensor_copy(picked2[:], tab[a][:].indirect(list2[:]))
             v2.append(picked2)
-            picked = held([P, S], U32, f"v_{a}")
-            nc.vector.tensor_copy(picked[:], tab[a][:].indirect(list1[:]))
-            v.append(picked)
+            if a == 0:
+                picked = held([P, S], U32, "v_0")
+                nc.vector.tensor_copy(picked[:], tab[a][:].indirect(list1[:]))
+                v.append([picked[:, :HALF], picked[:, HALF:]])
+            else:
+                picked = held([P, HALF], U32, "v_1")
+                nc.vector.tensor_copy(picked[:], tab[a][:].indirect(list1[:, : HALF // 16]))
+                v.append([picked[:]])
 
-        grouped = [[shared.tile([P, PACK, P, PACK], BF16, name=f"wg{b}{a}", align_bytes=64, offset=53248 + 4096 * (2 * b + 1 - a)) for a in range(PASSES)] for b in range(PASSES)]
+        grouped = [[shared.tile([P, PACK, P, PACK], BF16, name=f"wg{b}{a}", align_bytes=64, offset=55296 + 4096 * (2 * b + 1 - a)) for a in range(PASSES)] for b in range(PASSES)]
         w1_codes = [[held([P, KP], U32, f"wc{b}{a}") for a in range(PASSES)] for b in range(PASSES)]
         w1_plane = [[held([P, KP], U8, f"ws{b}{a}") for a in range(PASSES)] for b in range(PASSES)]
 
@@ -178,7 +183,6 @@ def tile_list_graft_mismatch_score_kernel(
 
         def first_product(i):
             b, c = steps[i]
-            cols = slice(CHUNK * c, CHUNK * (c + 1))
             gelu = ring.tile([P, 2, CHUNK, 2], F32, name="gelu")
             gelus[i] = gelu
             for u in range(2):
@@ -190,7 +194,7 @@ def tile_list_graft_mismatch_score_kernel(
                             out=bank[:, e, :],
                             lhsT=w1_codes[b][a][:, rows].bitcast(FP8X4),
                             lhsT_scale=w1_plane[b][a][:, rows],
-                            rhs=v[a][:, cols].bitcast(FP8X4),
+                            rhs=v[a][c // 2][:, CHUNK * (c % 2) : CHUNK * (c % 2 + 1)].bitcast(FP8X4),
                             rhs_scale=planes[a][:, S2 + CHUNK * c : S2 + CHUNK * (c + 1)],
                             start=(a == 0),
                             stop=(a == PASSES - 1),
@@ -221,32 +225,38 @@ def tile_list_graft_mismatch_score_kernel(
             for m in range(MT):
                 f_passes(0, m, f"acc{m}", (a,))
         cast_w1(False, 0, 0, raw00, 0, 0, 128)
-        raw1 = [load_w1(1, 0, 0, 512)]
+        raw1 = [load_w1(1, 0, 0, 512, 16384)]
         quantize_w1(0, 0, 0, 4)
         cast_w1(False, 0, 1, raw01[0], 0, 0, 64)
-        cast_w1(False, 0, 1, raw01[1], 256, 64, 92)
-        cast_w1(True, 0, 1, raw01[1], 256, 92, 128)
-        raw1.append(load_w1(1, 1, 0, 512))
+        cast_w1(False, 0, 1, raw01[1], 256, 64, 88)
+        cast_w1(True, 0, 1, raw01[1], 256, 88, 128)
+        raw1.append(load_w1(1, 1, 0, 512, 30720))
         quantize_w1(0, 1, 0, 2)
         quantize_w1(0, 1, 2, 4)
         w4.append(load_w4(1))
+        late = shared.tile([P, HALF], U32, name="v_1_late", align_bytes=64, offset=55296 + 2048)
+        nc.vector.tensor_copy(late[:], tab[1][:].indirect(list1[:, HALF // 16 :]))
+        v[1].append(late[:])
 
         first_product(0)
-        cast_w1(True, 1, 0, raw1[0], 0, 0, 48)
+        cast_w1(True, 1, 0, raw1[0], 0, 0, 56)
         first_product(1)
-        cast_w1(False, 1, 0, raw1[0], 0, 48, 128)
+        cast_w1(False, 1, 0, raw1[0], 0, 56, 128)
         scale_h(0)
         first_product(2)
         scale_h(1)
         quantize_h(0)
         quantize_w1(1, 0, 0, 4)
-        cast_w1(False, 1, 1, raw1[1], 0, 48, 128)
-        cast_w1(True, 1, 1, raw1[1], 0, 0, 48)
+        cast_w1(False, 1, 1, raw1[1], 0, 56, 128)
+        cast_w1(True, 1, 1, raw1[1], 0, 0, 56)
         quantize_h(1)
         first_product(3)
         f_passes(1, 0, "ring3")
         scale_h(2)
         quantize_w1(1, 1, 0, 4)
+        urg_sb = shared.tile([P, MT], F32, name="urg_sb", align_bytes=64, offset=55296 + 8192)
+        with nc.allow_non_contiguous_dma(reason="one urgency value for each partition"):
+            nc.sync.dma_start(urg_sb[:], urg.rearrange("(m p) -> p m", p=P))
         for m in range(MT):
             e_pass(0, m, 0, 0, HALF, False)
         first_product(4)

@@ -20,9 +20,20 @@ P = 128
 PACK = 4
 KP = P * PACK
 PASSES = K // KP
-HALF = 512
-CHUNK = 256
-MT = S2 // P
+HALF = S // 2
+QUARTER = S // 4
+FP4_N = 128
+PAIRS = S2 // (2 * P)
+RING = 4
+
+SCALAR_M_FIRST = 96
+
+AT_TAB = (0, 16384)
+AT_W1_01 = (0, 4096)
+AT_W1_1 = (8192, 16384)
+AT_W4_LAST = 16384 + 8192
+AT_URG = AT_W4_LAST + 2048
+AT_GELU_FIRST = 32768
 
 
 def tile_list_graft_mismatch_score_kernel(
@@ -31,261 +42,271 @@ def tile_list_graft_mismatch_score_kernel(
     nc = tc.nc
     with ExitStack() as ctx:
         keep = ctx.enter_context(tc.tile_pool(name="keep", bufs=1))
-        shared = ctx.enter_context(tc.tile_pool(name="shared", bufs=1))
-        ring = ctx.enter_context(tc.tile_pool(name="ring", bufs=4))
+        staging = ctx.enter_context(tc.tile_pool(name="staging", bufs=1))
+        ring = ctx.enter_context(tc.tile_pool(name="ring", bufs=RING))
         psum = ctx.enter_context(tc.psum_pool(name="psum", bufs=1))
 
-        def held(shape, dtype, name):
+        def kept(shape, dtype, name):
             return keep.tile(shape, dtype, name=name, align_bytes=64)
 
+        def staged(shape, dtype, name, offset):
+            return staging.tile(shape, dtype, name=name, align_bytes=64, offset=offset)
+
+        scale_rows = kept([P, T], U8, "scale_rows")
+        nc.sync.dma_start(
+            scale_rows[0:32, :].bitcast(I32), tab_scales.rearrange("a q t -> (a q) t").bitcast(I32)
+        )
+        nc.vector.memset(scale_rows[32:64, :].bitcast(I32), 0)
+        nc.vector.memset(scale_rows[64:P, :].bitcast(I32), 0)
         list2 = keep.tile([P, S2 // 16], U16, name="list2")
         nc.sync.dma_start(list2[:], offs2)
         list1 = keep.tile([P, S // 16], U16, name="list1")
         nc.sync.dma_start(list1[:], offs)
+        gain_sb = kept([P, PASSES, PACK], F32, "gain_sb")
+        nc.sync.dma_start(gain_sb[:], gain.rearrange("(b p t) -> p b t", p=P, t=PACK))
 
-        scale_rows = shared.tile([P, T], U8, name="scale_rows", align_bytes=64, offset=28672)
-        nc.vector.memset(scale_rows[:].bitcast(I32), 0)
-        by_row = tab_scales.rearrange("a (q r) t -> r q a t", r=4)
-        for r in range(4):
-            nc.scalar.dma_start(scale_rows[r:P:16, :].bitcast(I32), by_row[r].bitcast(I32))
-        w4_plane = held([P, PASSES, S], U8, "w4_plane")
+        w4_plane = kept([P, PASSES, S], U8, "w4_plane")
         nc.gpsimd.memset(w4_plane[:].rearrange("p a n -> p (a n)").bitcast(I32), 0)
-        plane1 = held([P, S2 + S], U8, "plane1")
-        nc.vector.memset(plane1[:].bitcast(I32), 0)
-        warm = shared.tile([P, 32], F32, name="warm", align_bytes=64, offset=16384 - 64)
-        nc.vector.memset(warm[:], 0.0)
-        warm_out = held([P, 32], F32, "warm_out")
-        nc.scalar.activation(warm_out[:], warm[:], ACT.Gelu_apprx_tanh)
-
-        gain_sb = held([P, PASSES, PACK], F32, "gain_sb")
-        nc.scalar.dma_start(gain_sb[:], gain.rearrange("(b p t) -> p b t", p=P, t=PACK))
-        neg_gain = held([P, PASSES, 2, 2], F32, "neg_gain")
-        nc.scalar.activation(
-            neg_gain[:].rearrange("p b u e -> p b (u e)"), gain_sb[:], ACT.Copy, scale=-1.0
-        )
-
         for q in range(4):
             nc.gpsimd.dma_start(
                 w4_plane[32 * q : 32 * q + 4, :, :].bitcast(I32),
                 w4_scales[:, 4 * q : 4 * q + 4, :].rearrange("a r n -> r a n").bitcast(I32),
             )
 
-        def load_w4(h):
-            words = shared.tile([P, PASSES, 2 * HALF], U8, name=f"w4_{h}", align_bytes=64, offset=55296 if h else 24576)
-            nc.sync.dma_start(
-                words[:].bitcast(I32),
-                w4_words[:, :, 2 * HALF * h : 2 * HALF * (h + 1)].rearrange("a p n -> p a n").bitcast(I32),
-            )
-            return words
-
-        def load_w1(b, a, c0, width, offset):
-            raw = shared.tile([P, PACK, width], F32, name=f"w1_{b}_{a}_{c0}", align_bytes=64, offset=offset)
-            src = w1[KP * a : KP * (a + 1), KP * b + c0 : KP * b + c0 + width]
-            nc.sync.dma_start(raw[:], src.rearrange("(p j) c -> p j c", j=PACK))
-            return raw
+        planes = [kept([P, S2 + S], U8, f"plane{a}") for a in range(PASSES)]
+        for a in range(PASSES):
+            nc.vector.memset(planes[a][:].bitcast(I32), 0)
 
         def load_tab(a):
-            words = shared.tile([P, T], U32, name=f"tab{a}", align_bytes=64, offset=38912 * (1 - a))
-            nc.sync.dma_start(
-                words[:].bitcast(I32), tab_words[a].rearrange("p t i -> p (t i)").bitcast(I32)
-            )
+            words = staged([P, T], U32, f"tab{a}", AT_TAB[a])
+            nc.sync.dma_start(words[:].bitcast(I32), tab_words[a].rearrange("p t i -> p (t i)").bitcast(I32))
             return words
 
-        tab = [load_tab(0)]
-        w4 = [load_w4(0)]
-        raw00 = load_w1(0, 0, 0, 512, 16384)
-        tab.append(load_tab(1))
+        def load_w4(half, words):
+            src = w4_words[:, :, 2 * HALF * half : 2 * HALF * (half + 1)]
+            nc.sync.dma_start(words[:].bitcast(I32), src.rearrange("a p n -> p a n").bitcast(I32))
+            return words
 
-        plane0 = held([P, S2 + S], U8, "plane0")
-        nc.vector.tensor_copy(plane0[:, :S2], scale_rows[:].indirect(list2[:]))
-        nc.vector.tensor_copy(plane0[:, S2:], scale_rows[:].indirect(list1[:]))
-        nc.sync.dma_start(plane1[0:112, :].bitcast(I32), plane0[16:128, :].bitcast(I32))
-        planes = [plane0, plane1]
-        raw01 = [load_w1(0, 1, 0, 256, 26624), load_w1(0, 1, 256, 256, 30720)]
+        def load_w1(b, a, c0, raw):
+            src = w1[KP * a : KP * (a + 1), KP * b + c0 : KP * b + c0 + raw.shape[2]]
+            nc.sync.dma_start(raw[:], src.rearrange("(p i) c -> p i c", i=PACK))
+            return raw
+
+        tab = [load_tab(a) for a in range(PASSES)]
+        w4 = [load_w4(0, kept([P, PASSES, 2 * HALF], U8, "w4_first"))]
+        raw00 = load_w1(0, 0, 0, kept([P, PACK, KP], F32, "raw00"))
+
+        picked_rows = kept([P, S2 + S], U8, "picked_rows")
+        nc.vector.tensor_copy(picked_rows[:, :S2], scale_rows[:].indirect(list2[:]))
+        nc.vector.tensor_copy(picked_rows[:, S2:], scale_rows[:].indirect(list1[:]))
+        for a, queue in enumerate((nc.scalar, nc.gpsimd)):
+            for q in range(4):
+                queue.dma_start(
+                    planes[a][32 * q : 32 * q + 4, :].bitcast(I32),
+                    picked_rows[16 * a + 4 * q : 16 * a + 4 * q + 4, :].bitcast(I32),
+                )
+
         v, v2 = [], []
         for a in range(PASSES):
-            picked2 = held([P, S2], U32, f"v2_{a}")
-            nc.vector.tensor_copy(picked2[:], tab[a][:].indirect(list2[:]))
-            v2.append(picked2)
-            if a == 0:
-                picked = held([P, S], U32, "v_0")
-                nc.vector.tensor_copy(picked[:], tab[a][:].indirect(list1[:]))
-                v.append([picked[:, :HALF], picked[:, HALF:]])
-            else:
-                picked = held([P, HALF], U32, "v_1")
-                nc.vector.tensor_copy(picked[:], tab[a][:].indirect(list1[:, : HALF // 16]))
-                v.append([picked[:]])
+            v2.append(kept([P, S2], U32, f"v2_{a}"))
+            nc.vector.tensor_copy(v2[a][:], tab[a][:].indirect(list2[:]))
+            v.append(kept([P, S], U32, f"v_{a}"))
+            nc.vector.tensor_copy(v[a][:], tab[a][:].indirect(list1[:]))
 
-        grouped = [[shared.tile([P, PACK, P, PACK], BF16, name=f"wg{b}{a}", align_bytes=64, offset=55296 + 4096 * (2 * b + 1 - a)) for a in range(PASSES)] for b in range(PASSES)]
-        w1_codes = [[held([P, KP], U32, f"wc{b}{a}") for a in range(PASSES)] for b in range(PASSES)]
-        w1_plane = [[held([P, KP], U8, f"ws{b}{a}") for a in range(PASSES)] for b in range(PASSES)]
+        raw01 = [
+            load_w1(0, 1, KP // 2 * half, staged([P, PACK, KP // 2], F32, f"raw01_{half}", AT_W1_01[half]))
+            for half in range(2)
+        ]
+        raw1 = [load_w1(1, a, 0, staged([P, PACK, KP], F32, f"raw1{a}", AT_W1_1[a])) for a in range(PASSES)]
+        w4.append(load_w4(1, staged([P, PASSES, 2 * HALF], U8, "w4_last", AT_W4_LAST)))
+        urg_sb = staged([P, 2 * PAIRS], F32, "urg_sb", AT_URG)
+        with nc.allow_non_contiguous_dma(reason="one urgency value for each partition"):
+            nc.sync.dma_start(urg_sb[:], urg.rearrange("(m p) -> p m", p=P))
 
-        def cast_w1(on_vector, b, a, raw, c0, m0, m1):
-            dst = grouped[b][a][:, :, m0:m1, :].rearrange("p t m j -> p m t j")
-            src = raw[:, :, PACK * m0 - c0 : PACK * m1 - c0].rearrange("p j (m t) -> p m t j", t=PACK)
-            if on_vector:
-                nc.vector.tensor_copy(dst, src)
-            else:
-                nc.scalar.copy(dst, src)
+        neg_gain = kept([P, PASSES, 2, 2], F32, "neg_gain")
+        nc.vector.tensor_scalar(neg_gain[:].rearrange("p b u e -> p b (u e)"), gain_sb[:], -1.0, None, MULT)
+
+        tiles = [(b, a) for b in range(PASSES) for a in range(PASSES)]
+        w1_bf = {(b, a): kept([P, PACK, P, PACK], BF16, f"w1_bf{b}{a}") for b, a in tiles[:-1]}
+        w1_bf[1, 1] = staged([P, PACK, P, PACK], BF16, "w1_bf11", AT_GELU_FIRST)
+        w1_codes = {(b, a): kept([P, KP], U32, f"w1_codes{b}{a}") for b, a in tiles}
+        w1_plane = {(b, a): kept([P, KP], U8, f"w1_plane{b}{a}") for b, a in tiles}
+
+        def round_w1(copy, b, a, raw, c0, m0, m1):
+            dst = w1_bf[b, a][:, :, m0:m1, :].rearrange("p t m i -> p m t i")
+            src = raw[:, :, PACK * m0 - c0 : PACK * m1 - c0].rearrange("p i (m t) -> p m t i", t=PACK)
+            copy(dst, src)
 
         def quantize_w1(b, a, t0, t1):
             nc.vector.quantize_mx(
-                out=w1_codes[b][a][:, P * t0 : P * t1].bitcast(FP8X4),
-                scales=w1_plane[b][a][:, P * t0 : P * t1],
-                in_=grouped[b][a][:, t0:t1].rearrange("p t m j -> p (t m j)"),
+                out=w1_codes[b, a][:, P * t0 : P * t1].bitcast(FP8X4),
+                scales=w1_plane[b, a][:, P * t0 : P * t1],
+                in_=w1_bf[b, a][:, t0:t1].rearrange("p t m i -> p (t m i)"),
             )
 
-        h_codes = [[held([P, HALF], U32, f"hc{b}{h}") for h in range(2)] for b in range(PASSES)]
-        h_plane = [[held([P, HALF], U8, f"hs{b}{h}") for h in range(2)] for b in range(PASSES)]
-        acc = {}
+        steps = [(b, c) for b in range(PASSES) for c in range(S // QUARTER)]
+        x_banks, gelus, h_bf = {}, {}, {}
+        h_codes = {step: kept([P, QUARTER], U32, f"h_codes{step[0]}{step[1]}") for step in steps}
+        h_plane = {step: kept([P, QUARTER], U8, f"h_plane{step[0]}{step[1]}") for step in steps}
 
-        def f_passes(h, m, tag, passes=(0, 1)):
-            if passes[0] == 0:
-                acc[h, m] = psum.tile([P, HALF], F32, name=f"acc{h}{m}", tag=tag)
-            bank = acc[h, m]
-            cols = slice(P * m, P * (m + 1))
-            for a in passes:
+        def x_pass(i, u, a):
+            b, c = steps[i]
+            cols = slice(QUARTER * c, QUARTER * (c + 1))
+            plane_cols = slice(S2 + QUARTER * c, S2 + QUARTER * (c + 1))
+            if a == 0:
+                x_banks[i, u] = psum.tile([P, 2, QUARTER], F32, name="x", tag=f"x{(2 * i + u) % RING}")
+            for e in range(2):
+                rows = slice(P * (2 * u + e), P * (2 * u + e + 1))
                 nc.tensor.matmul_mx(
-                    out=bank[:],
-                    lhsT=v2[a][:, cols].bitcast(FP8X4),
-                    lhsT_scale=planes[a][:, cols],
-                    rhs=w4[h][:, a, :].bitcast(FP4X4),
-                    rhs_scale=w4_plane[:, a, HALF * h : HALF * (h + 1)],
-                    start=(a == 0),
-                    stop=False,
+                    out=x_banks[i, u][:, e, :],
+                    lhsT=w1_codes[b, a][:, rows].bitcast(FP8X4),
+                    lhsT_scale=w1_plane[b, a][:, rows],
+                    rhs=v[a][:, cols].bitcast(FP8X4),
+                    rhs_scale=planes[a][:, plane_cols],
+                    start=(a == 0 and e == 0),
+                    stop=(a == PASSES - 1 and e == 1),
                 )
 
-        def e_pass(h, m, b, n0, n1, stop):
-            cols = slice(P * m, P * (m + 1))
-            nc.tensor.matmul_mx(
-                out=acc[h, m][:, n0:n1],
-                lhsT=v2[b][:, cols].bitcast(FP8X4),
-                lhsT_scale=planes[b][:, cols],
-                rhs=h_codes[b][h][:, n0:n1].bitcast(FP8X4),
-                rhs_scale=h_plane[b][h][:, n0:n1],
-                start=False,
-                stop=stop,
+        def gelu_x(i, u):
+            if u == 0 and i == 0:
+                gelus[i] = staged([P, 2, QUARTER, 2], F32, "gelu_first", AT_GELU_FIRST)
+            elif u == 0:
+                gelus[i] = ring.tile([P, 2, QUARTER, 2], F32, name="gelu")
+            nc.scalar.activation(
+                gelus[i][:, u], x_banks[i, u][:].rearrange("p e n -> p n e"), ACT.Gelu_apprx_tanh
             )
 
-        squares = {}
-
-        def square(h, m):
-            squares[h, m] = held([P, HALF], F32, f"square{h}{m}")
-            nc.scalar.activation(squares[h, m][:], acc[h, m][:], ACT.Square)
-
-        def finish(h, m):
-            result = held([P, HALF], F32, f"result{h}{m}")
-            nc.vector.tensor_scalar(result[:], squares[h, m][:], urg_sb[:, m : m + 1], None, MULT)
-            nc.sync.dma_start(out[P * m : P * (m + 1), HALF * h : HALF * (h + 1)], result[:])
-
-        steps = [(b, c) for b in range(PASSES) for c in range(S // CHUNK)]
-        gelus, scaled = {}, {}
-
         def first_product(i):
-            b, c = steps[i]
-            gelu = ring.tile([P, 2, CHUNK, 2], F32, name="gelu")
-            gelus[i] = gelu
             for u in range(2):
-                bank = psum.tile([P, 2, CHUNK], F32, name="x", tag=f"ring{(2 * i + u) % 4 if i < 4 else (2 * i + u - 8) % 3}")
-                for e in range(2):
-                    rows = slice(P * (2 * u + e), P * (2 * u + e + 1))
-                    for a in range(PASSES):
-                        nc.tensor.matmul_mx(
-                            out=bank[:, e, :],
-                            lhsT=w1_codes[b][a][:, rows].bitcast(FP8X4),
-                            lhsT_scale=w1_plane[b][a][:, rows],
-                            rhs=v[a][c // 2][:, CHUNK * (c % 2) : CHUNK * (c % 2 + 1)].bitcast(FP8X4),
-                            rhs_scale=planes[a][:, S2 + CHUNK * c : S2 + CHUNK * (c + 1)],
-                            start=(a == 0),
-                            stop=(a == PASSES - 1),
-                        )
-                nc.scalar.activation(gelu[:, u], bank[:].rearrange("p e n -> p n e"), ACT.Gelu_apprx_tanh)
+                for a in range(PASSES):
+                    x_pass(i, u, a)
+                gelu_x(i, u)
 
         def scale_h(i):
             b = steps[i][0]
-            h_bf = ring.tile([P, CHUNK, 2, 2], BF16, name="h_bf", align_bytes=64)
-            scaled[i] = h_bf
+            h_bf[i] = ring.tile([P, QUARTER, 2, 2], BF16, name="h_bf", align_bytes=64)
             nc.vector.tensor_tensor(
-                h_bf[:],
+                h_bf[i][:],
                 gelus[i][:].rearrange("p u n e -> p n u e"),
-                neg_gain[:, b : b + 1].to_broadcast([P, CHUNK, 2, 2]),
+                neg_gain[:, b : b + 1].to_broadcast([P, QUARTER, 2, 2]),
                 MULT,
             )
 
         def quantize_h(i):
-            b, c = steps[i]
-            cols = slice(CHUNK * (c % 2), CHUNK * (c % 2 + 1))
             nc.vector.quantize_mx(
-                out=h_codes[b][c // 2][:, cols].bitcast(FP8X4),
-                scales=h_plane[b][c // 2][:, cols],
-                in_=scaled[i][:].rearrange("p n u e -> p (n u e)"),
+                out=h_codes[steps[i]][:].bitcast(FP8X4),
+                scales=h_plane[steps[i]][:],
+                in_=h_bf[i][:].rearrange("p n u e -> p (n u e)"),
             )
 
-        for a in range(PASSES):
-            for m in range(MT):
-                f_passes(0, m, f"acc{m}", (a,))
-        cast_w1(False, 0, 0, raw00, 0, 0, 128)
-        raw1 = [load_w1(1, 0, 0, 512, 16384)]
-        quantize_w1(0, 0, 0, 4)
-        cast_w1(False, 0, 1, raw01[0], 0, 0, 64)
-        cast_w1(False, 0, 1, raw01[1], 256, 64, 88)
-        cast_w1(True, 0, 1, raw01[1], 256, 88, 128)
-        raw1.append(load_w1(1, 1, 0, 512, 30720))
-        quantize_w1(0, 1, 0, 2)
-        quantize_w1(0, 1, 2, 4)
-        w4.append(load_w4(1))
-        late = shared.tile([P, HALF], U32, name="v_1_late", align_bytes=64, offset=55296 + 2048)
-        nc.vector.tensor_copy(late[:], tab[1][:].indirect(list1[:, HALF // 16 :]))
-        v[1].append(late[:])
+        diff, squares = {}, {}
 
-        first_product(0)
-        cast_w1(True, 1, 0, raw1[0], 0, 0, 56)
-        first_product(1)
-        cast_w1(False, 1, 0, raw1[0], 0, 56, 128)
+        def f_pass(c, a):
+            for g in range(PAIRS):
+                if a == 0:
+                    diff[c, g] = psum.tile([P, 2, QUARTER], F32, name="diff", tag=f"diff{c % 2}{g}")
+                for e in range(2):
+                    rows = slice(P * (2 * g + e), P * (2 * g + e + 1))
+                    for n0 in range(0, QUARTER, FP4_N):
+                        j0 = QUARTER * c + n0
+                        nc.tensor.matmul_mx(
+                            out=diff[c, g][:, e, n0 : n0 + FP4_N],
+                            lhsT=v2[a][:, rows].bitcast(FP8X4),
+                            lhsT_scale=planes[a][:, rows],
+                            rhs=w4[c // 2][:, a, 2 * (j0 % HALF) : 2 * (j0 % HALF + FP4_N)].bitcast(FP4X4),
+                            rhs_scale=w4_plane[:, a, j0 : j0 + FP4_N],
+                            start=(a == 0 and e == 0 and n0 == 0),
+                            stop=False,
+                        )
+
+        def f_product(c):
+            for a in range(PASSES):
+                f_pass(c, a)
+
+        def e_pass(i):
+            b, c = steps[i]
+            for g in range(PAIRS):
+                for e in range(2):
+                    rows = slice(P * (2 * g + e), P * (2 * g + e + 1))
+                    nc.tensor.matmul_mx(
+                        out=diff[c, g][:, e, :],
+                        lhsT=v2[b][:, rows].bitcast(FP8X4),
+                        lhsT_scale=planes[b][:, rows],
+                        rhs=h_codes[b, c][:].bitcast(FP8X4),
+                        rhs_scale=h_plane[b, c][:],
+                        start=False,
+                        stop=(b == PASSES - 1 and e == 1),
+                    )
+
+        def square(c):
+            for g in range(PAIRS):
+                squares[c, g] = kept([P, 2, QUARTER], F32, f"square{c}{g}")
+                nc.scalar.activation(squares[c, g][:], diff[c, g][:], ACT.Square)
+
+        def finish(c, g):
+            result = kept([P, 2, QUARTER], F32, f"result{c}{g}")
+            for e in range(2):
+                m = 2 * g + e
+                nc.vector.tensor_scalar(result[:, e], squares[c, g][:, e], urg_sb[:, m : m + 1], None, MULT)
+            dst = out[2 * P * g : 2 * P * (g + 1), QUARTER * c : QUARTER * (c + 1)]
+            nc.sync.dma_start(dst.rearrange("(e p) n -> p e n", p=P), result[:])
+
+        round_w1(nc.scalar.copy, 0, 0, raw00, 0, 0, SCALAR_M_FIRST)
+        round_w1(nc.vector.tensor_copy, 0, 0, raw00, 0, SCALAR_M_FIRST, P)
+        round_w1(nc.vector.tensor_copy, 0, 1, raw01[0], 0, 0, P // 2)
+        quantize_w1(0, 0, 0, PACK)
+        round_w1(nc.vector.tensor_copy, 0, 1, raw01[1], KP // 2, P // 2, P)
+        quantize_w1(0, 1, 0, 2)
+        quantize_w1(0, 1, 2, PACK)
+        for i in range(2):
+            for u in range(2):
+                x_pass(i, u, 0)
+
+        for i in range(2):
+            for u in range(2):
+                x_pass(i, u, 1)
+                gelu_x(i, u)
+        for a in range(PASSES):
+            for c in range(2):
+                f_pass(c, a)
+        round_w1(nc.vector.tensor_copy, 1, 0, raw1[0], 0, 0, P)
         scale_h(0)
+        quantize_w1(1, 0, 0, PACK)
         first_product(2)
+        round_w1(nc.scalar.copy, 1, 1, raw1[1], 0, 0, P)
         scale_h(1)
         quantize_h(0)
-        quantize_w1(1, 0, 0, 4)
-        cast_w1(False, 1, 1, raw1[1], 0, 56, 128)
-        cast_w1(True, 1, 1, raw1[1], 0, 0, 56)
-        quantize_h(1)
         first_product(3)
-        f_passes(1, 0, "ring3")
+        e_pass(0)
         scale_h(2)
-        quantize_w1(1, 1, 0, 4)
-        urg_sb = shared.tile([P, MT], F32, name="urg_sb", align_bytes=64, offset=55296 + 8192)
-        with nc.allow_non_contiguous_dma(reason="one urgency value for each partition"):
-            nc.sync.dma_start(urg_sb[:], urg.rearrange("(m p) -> p m", p=P))
-        for m in range(MT):
-            e_pass(0, m, 0, 0, HALF, False)
+        quantize_h(1)
+        quantize_w1(1, 1, 0, PACK)
+        e_pass(1)
         first_product(4)
         scale_h(3)
         quantize_h(2)
         first_product(5)
+
         scale_h(4)
         quantize_h(3)
-        first_product(6)
-        e_pass(1, 0, 0, 0, HALF, False)
-        scale_h(5)
         quantize_h(4)
+        first_product(6)
+        e_pass(4)
         first_product(7)
+        square(0)
+        scale_h(5)
         quantize_h(5)
-        for m in range(MT):
-            e_pass(0, m, 1, 0, HALF, True)
-            square(0, m)
-        scale_h(6)
-        for m in range(1, MT):
-            f_passes(1, m, f"ring{(m + 1) % 3}")
-            e_pass(1, m, 0, 0, HALF, False)
-        scale_h(7)
-        quantize_h(6)
-        for m in range(MT):
-            e_pass(1, m, 1, 0, CHUNK, False)
-        quantize_h(7)
-        for m in range(MT):
-            e_pass(1, m, 1, CHUNK, HALF, True)
-            square(1, m)
-        for h in range(2):
-            for m in range(MT):
-                finish(h, m)
+        e_pass(5)
+        square(1)
+        for c in (2, 3):
+            f_product(c)
+            e_pass(c)
+            scale_h(c + 4)
+            for g in range(PAIRS):
+                finish(c - 2, g)
+            quantize_h(c + 4)
+            e_pass(c + 4)
+            square(c)
+        for c in (2, 3):
+            for g in range(PAIRS):
+                finish(c, g)

from contextlib import ExitStack

import concourse.mybir as mybir

K, T, S, S2 = 1024, 4096, 1024, 512
FLOPS = 2 * K * K * S + 2 * 2 * K * S2 * S

F32 = mybir.dt.float32
BF16 = mybir.dt.bfloat16
I32 = mybir.dt.int32
U32 = mybir.dt.uint32
U16 = mybir.dt.uint16
U8 = mybir.dt.uint8
FP8X4 = mybir.dt.float8_e4m3fn_x4
FP4X4 = mybir.dt.float4_e2m1fn_x4
ACT = mybir.ActivationFunctionType
MULT = mybir.AluOpType.mult

P = 128
PACK = 4
KP = P * PACK
PASSES = K // KP
HALF = S // 2
QUARTER = S // 4
FP4_N = 128
PAIRS = S2 // (2 * P)
RING = 4

SCALAR_M_FIRST = 96

AT_TAB = (0, 16384)
AT_W1_01 = (0, 4096)
AT_W1_1 = (8192, 16384)
AT_W4_LAST = 16384 + 8192
AT_URG = AT_W4_LAST + 2048
AT_GELU_FIRST = 32768


def tile_list_graft_mismatch_score_kernel(
    tc, tab_words, tab_scales, offs, offs2, w1, gain, w4_words, w4_scales, urg, out
):
    nc = tc.nc
    with ExitStack() as ctx:
        keep = ctx.enter_context(tc.tile_pool(name="keep", bufs=1))
        staging = ctx.enter_context(tc.tile_pool(name="staging", bufs=1))
        ring = ctx.enter_context(tc.tile_pool(name="ring", bufs=RING))
        psum = ctx.enter_context(tc.psum_pool(name="psum", bufs=1))

        def kept(shape, dtype, name):
            return keep.tile(shape, dtype, name=name, align_bytes=64)

        def staged(shape, dtype, name, offset):
            return staging.tile(shape, dtype, name=name, align_bytes=64, offset=offset)

        scale_rows = kept([P, T], U8, "scale_rows")
        nc.sync.dma_start(
            scale_rows[0:32, :].bitcast(I32), tab_scales.rearrange("a q t -> (a q) t").bitcast(I32)
        )
        nc.vector.memset(scale_rows[32:64, :].bitcast(I32), 0)
        nc.vector.memset(scale_rows[64:P, :].bitcast(I32), 0)
        list2 = keep.tile([P, S2 // 16], U16, name="list2")
        nc.sync.dma_start(list2[:], offs2)
        list1 = keep.tile([P, S // 16], U16, name="list1")
        nc.sync.dma_start(list1[:], offs)
        gain_sb = kept([P, PASSES, PACK], F32, "gain_sb")
        nc.sync.dma_start(gain_sb[:], gain.rearrange("(b p t) -> p b t", p=P, t=PACK))

        w4_plane = kept([P, PASSES, S], U8, "w4_plane")
        nc.gpsimd.memset(w4_plane[:].rearrange("p a n -> p (a n)").bitcast(I32), 0)
        for q in range(4):
            nc.gpsimd.dma_start(
                w4_plane[32 * q : 32 * q + 4, :, :].bitcast(I32),
                w4_scales[:, 4 * q : 4 * q + 4, :].rearrange("a r n -> r a n").bitcast(I32),
            )

        planes = [kept([P, S2 + S], U8, f"plane{a}") for a in range(PASSES)]
        for a in range(PASSES):
            nc.vector.memset(planes[a][:].bitcast(I32), 0)

        def load_tab(a):
            words = staged([P, T], U32, f"tab{a}", AT_TAB[a])
            nc.sync.dma_start(words[:].bitcast(I32), tab_words[a].rearrange("p t i -> p (t i)").bitcast(I32))
            return words

        def load_w4(half, words):
            src = w4_words[:, :, 2 * HALF * half : 2 * HALF * (half + 1)]
            nc.sync.dma_start(words[:].bitcast(I32), src.rearrange("a p n -> p a n").bitcast(I32))
            return words

        def load_w1(b, a, c0, raw):
            src = w1[KP * a : KP * (a + 1), KP * b + c0 : KP * b + c0 + raw.shape[2]]
            nc.sync.dma_start(raw[:], src.rearrange("(p i) c -> p i c", i=PACK))
            return raw

        tab = [load_tab(a) for a in range(PASSES)]
        w4 = [load_w4(0, kept([P, PASSES, 2 * HALF], U8, "w4_first"))]
        raw00 = load_w1(0, 0, 0, kept([P, PACK, KP], F32, "raw00"))

        picked_rows = kept([P, S2 + S], U8, "picked_rows")
        nc.vector.tensor_copy(picked_rows[:, :S2], scale_rows[:].indirect(list2[:]))
        nc.vector.tensor_copy(picked_rows[:, S2:], scale_rows[:].indirect(list1[:]))
        for a, queue in enumerate((nc.scalar, nc.gpsimd)):
            for q in range(4):
                queue.dma_start(
                    planes[a][32 * q : 32 * q + 4, :].bitcast(I32),
                    picked_rows[16 * a + 4 * q : 16 * a + 4 * q + 4, :].bitcast(I32),
                )

        v, v2 = [], []
        for a in range(PASSES):
            v2.append(kept([P, S2], U32, f"v2_{a}"))
            nc.vector.tensor_copy(v2[a][:], tab[a][:].indirect(list2[:]))
            v.append(kept([P, S], U32, f"v_{a}"))
            nc.vector.tensor_copy(v[a][:], tab[a][:].indirect(list1[:]))

        raw01 = [
            load_w1(0, 1, KP // 2 * half, staged([P, PACK, KP // 2], F32, f"raw01_{half}", AT_W1_01[half]))
            for half in range(2)
        ]
        raw1 = [load_w1(1, a, 0, staged([P, PACK, KP], F32, f"raw1{a}", AT_W1_1[a])) for a in range(PASSES)]
        w4.append(load_w4(1, staged([P, PASSES, 2 * HALF], U8, "w4_last", AT_W4_LAST)))
        urg_sb = staged([P, 2 * PAIRS], F32, "urg_sb", AT_URG)
        with nc.allow_non_contiguous_dma(reason="one urgency value for each partition"):
            nc.sync.dma_start(urg_sb[:], urg.rearrange("(m p) -> p m", p=P))

        neg_gain = kept([P, PASSES, 2, 2], F32, "neg_gain")
        nc.vector.tensor_scalar(neg_gain[:].rearrange("p b u e -> p b (u e)"), gain_sb[:], -1.0, None, MULT)

        tiles = [(b, a) for b in range(PASSES) for a in range(PASSES)]
        w1_bf = {(b, a): kept([P, PACK, P, PACK], BF16, f"w1_bf{b}{a}") for b, a in tiles[:-1]}
        w1_bf[1, 1] = staged([P, PACK, P, PACK], BF16, "w1_bf11", AT_GELU_FIRST)
        w1_codes = {(b, a): kept([P, KP], U32, f"w1_codes{b}{a}") for b, a in tiles}
        w1_plane = {(b, a): kept([P, KP], U8, f"w1_plane{b}{a}") for b, a in tiles}

        def round_w1(copy, b, a, raw, c0, m0, m1):
            dst = w1_bf[b, a][:, :, m0:m1, :].rearrange("p t m i -> p m t i")
            src = raw[:, :, PACK * m0 - c0 : PACK * m1 - c0].rearrange("p i (m t) -> p m t i", t=PACK)
            copy(dst, src)

        def quantize_w1(b, a, t0, t1):
            nc.vector.quantize_mx(
                out=w1_codes[b, a][:, P * t0 : P * t1].bitcast(FP8X4),
                scales=w1_plane[b, a][:, P * t0 : P * t1],
                in_=w1_bf[b, a][:, t0:t1].rearrange("p t m i -> p (t m i)"),
            )

        steps = [(b, c) for b in range(PASSES) for c in range(S // QUARTER)]
        x_banks, gelus, h_bf = {}, {}, {}
        h_codes = {step: kept([P, QUARTER], U32, f"h_codes{step[0]}{step[1]}") for step in steps}
        h_plane = {step: kept([P, QUARTER], U8, f"h_plane{step[0]}{step[1]}") for step in steps}

        def x_pass(i, u, a):
            b, c = steps[i]
            cols = slice(QUARTER * c, QUARTER * (c + 1))
            plane_cols = slice(S2 + QUARTER * c, S2 + QUARTER * (c + 1))
            if a == 0:
                x_banks[i, u] = psum.tile([P, 2, QUARTER], F32, name="x", tag=f"x{(2 * i + u) % RING}")
            for e in range(2):
                rows = slice(P * (2 * u + e), P * (2 * u + e + 1))
                nc.tensor.matmul_mx(
                    out=x_banks[i, u][:, e, :],
                    lhsT=w1_codes[b, a][:, rows].bitcast(FP8X4),
                    lhsT_scale=w1_plane[b, a][:, rows],
                    rhs=v[a][:, cols].bitcast(FP8X4),
                    rhs_scale=planes[a][:, plane_cols],
                    start=(a == 0 and e == 0),
                    stop=(a == PASSES - 1 and e == 1),
                )

        def gelu_x(i, u):
            if u == 0 and i == 0:
                gelus[i] = staged([P, 2, QUARTER, 2], F32, "gelu_first", AT_GELU_FIRST)
            elif u == 0:
                gelus[i] = ring.tile([P, 2, QUARTER, 2], F32, name="gelu")
            nc.scalar.activation(
                gelus[i][:, u], x_banks[i, u][:].rearrange("p e n -> p n e"), ACT.Gelu_apprx_tanh
            )

        def first_product(i):
            for u in range(2):
                for a in range(PASSES):
                    x_pass(i, u, a)
                gelu_x(i, u)

        def scale_h(i):
            b = steps[i][0]
            h_bf[i] = ring.tile([P, QUARTER, 2, 2], BF16, name="h_bf", align_bytes=64)
            nc.vector.tensor_tensor(
                h_bf[i][:],
                gelus[i][:].rearrange("p u n e -> p n u e"),
                neg_gain[:, b : b + 1].to_broadcast([P, QUARTER, 2, 2]),
                MULT,
            )

        def quantize_h(i):
            nc.vector.quantize_mx(
                out=h_codes[steps[i]][:].bitcast(FP8X4),
                scales=h_plane[steps[i]][:],
                in_=h_bf[i][:].rearrange("p n u e -> p (n u e)"),
            )

        diff, squares = {}, {}

        def f_pass(c, a):
            for g in range(PAIRS):
                if a == 0:
                    diff[c, g] = psum.tile([P, 2, QUARTER], F32, name="diff", tag=f"diff{c % 2}{g}")
                for e in range(2):
                    rows = slice(P * (2 * g + e), P * (2 * g + e + 1))
                    for n0 in range(0, QUARTER, FP4_N):
                        j0 = QUARTER * c + n0
                        nc.tensor.matmul_mx(
                            out=diff[c, g][:, e, n0 : n0 + FP4_N],
                            lhsT=v2[a][:, rows].bitcast(FP8X4),
                            lhsT_scale=planes[a][:, rows],
                            rhs=w4[c // 2][:, a, 2 * (j0 % HALF) : 2 * (j0 % HALF + FP4_N)].bitcast(FP4X4),
                            rhs_scale=w4_plane[:, a, j0 : j0 + FP4_N],
                            start=(a == 0 and e == 0 and n0 == 0),
                            stop=False,
                        )

        def f_product(c):
            for a in range(PASSES):
                f_pass(c, a)

        def e_pass(i):
            b, c = steps[i]
            for g in range(PAIRS):
                for e in range(2):
                    rows = slice(P * (2 * g + e), P * (2 * g + e + 1))
                    nc.tensor.matmul_mx(
                        out=diff[c, g][:, e, :],
                        lhsT=v2[b][:, rows].bitcast(FP8X4),
                        lhsT_scale=planes[b][:, rows],
                        rhs=h_codes[b, c][:].bitcast(FP8X4),
                        rhs_scale=h_plane[b, c][:],
                        start=False,
                        stop=(b == PASSES - 1 and e == 1),
                    )

        def square(c):
            for g in range(PAIRS):
                squares[c, g] = kept([P, 2, QUARTER], F32, f"square{c}{g}")
                nc.scalar.activation(squares[c, g][:], diff[c, g][:], ACT.Square)

        def finish(c, g):
            result = kept([P, 2, QUARTER], F32, f"result{c}{g}")
            for e in range(2):
                m = 2 * g + e
                nc.vector.tensor_scalar(result[:, e], squares[c, g][:, e], urg_sb[:, m : m + 1], None, MULT)
            dst = out[2 * P * g : 2 * P * (g + 1), QUARTER * c : QUARTER * (c + 1)]
            nc.sync.dma_start(dst.rearrange("(e p) n -> p e n", p=P), result[:])

        round_w1(nc.scalar.copy, 0, 0, raw00, 0, 0, SCALAR_M_FIRST)
        round_w1(nc.vector.tensor_copy, 0, 0, raw00, 0, SCALAR_M_FIRST, P)
        round_w1(nc.vector.tensor_copy, 0, 1, raw01[0], 0, 0, P // 2)
        quantize_w1(0, 0, 0, PACK)
        round_w1(nc.vector.tensor_copy, 0, 1, raw01[1], KP // 2, P // 2, P)
        quantize_w1(0, 1, 0, 2)
        quantize_w1(0, 1, 2, PACK)
        for i in range(2):
            for u in range(2):
                x_pass(i, u, 0)

        for i in range(2):
            for u in range(2):
                x_pass(i, u, 1)
                gelu_x(i, u)
        for a in range(PASSES):
            for c in range(2):
                f_pass(c, a)
        round_w1(nc.vector.tensor_copy, 1, 0, raw1[0], 0, 0, P)
        scale_h(0)
        quantize_w1(1, 0, 0, PACK)
        first_product(2)
        round_w1(nc.scalar.copy, 1, 1, raw1[1], 0, 0, P)
        scale_h(1)
        quantize_h(0)
        first_product(3)
        e_pass(0)
        scale_h(2)
        quantize_h(1)
        quantize_w1(1, 1, 0, PACK)
        e_pass(1)
        first_product(4)
        scale_h(3)
        quantize_h(2)
        first_product(5)

        scale_h(4)
        quantize_h(3)
        quantize_h(4)
        first_product(6)
        e_pass(4)
        first_product(7)
        square(0)
        scale_h(5)
        quantize_h(5)
        e_pass(5)
        square(1)
        for c in (2, 3):
            f_product(c)
            e_pass(c)
            scale_h(c + 4)
            for g in range(PAIRS):
                finish(c - 2, g)
            quantize_h(c + 4)
            e_pass(c + 4)
            square(c)
        for c in (2, 3):
            for g in range(PAIRS):
                finish(c, g)
